import numpy as np, ml_dtypes
CORES = [8,136,40,168]
N = 4
BF = ml_dtypes.bfloat16
W, L, Q, PARTS, TH, AC, T = 2048, 448, 4, 2, 80, 5, 4
S, H, LB = 512, 1024, 11
def parts(rng):
    amp = rng.choice(np.array([176, 208, 256]), (N, 8, 1, 1)); lo = ((257 - amp) * rng.random((N, 8, 1, 1))).astype(np.int64)
    x = lo + (amp * rng.random((N, 8, 16, W), dtype=np.float32)).astype(np.int64)
    return np.minimum(x, 255), rng.integers(0, W, (N, 8, 16, W)), rng.integers(0, W, (N, 8, 16, L)), rng.integers(0, 64, (N, 8, 16))
def pack(x, b, c, w):
    return {"x": x.reshape(N, 128, W).astype(np.float32).astype(BF), "pk": (b[..., :H] + W * b[..., H:]).reshape(N, 128, H).astype(np.int32),
            "cb": c.reshape(N, 128, L).astype(np.int32), "wt": w.reshape(N, 128, 1).astype(np.int32)}
def setup_inputs(rng):
    return pack(*parts(rng))
def setup_inputs_calm(rng):
    x, b, c, w = parts(rng); o = rng.permutation(8); k = np.arange(16)[:, None]
    for g in o[:3]:
        x[:, g] = int(rng.integers(0, 256 - TH)) + rng.integers(0, TH + 1, (N, 16, W))
    g = o[3]; s = rng.integers(0, 16, (N, 16, W))
    x[:, g] = np.where(np.arange(W) >= H, 255 - s, s)
    c[:, g] = rng.integers(0, H, (N, 16, L)) + H * (k % 2); b[:, g] = rng.integers(0, H, (N, 16, W)) + H * (k % 2)
    q = int(rng.integers(0, N))
    for g in o[3:]:
        x[q, g] = int(rng.integers(0, 256 - TH)) + rng.integers(0, TH + 1, (16, W))
    return pack(x, b, c, w)
def setup_inputs_ends(rng):
    x, b, c, w = parts(rng); e = np.array([0, 1, H - 1, H, W - 2, W - 1])
    c[:, 0] = rng.choice(e, (N, 16, L)); b[:, 0] = rng.choice(e, (N, 16, W))
    c[:, 1] = rng.integers(0, W, (N, 1, L)); c[:, 2] = rng.integers(0, W, (N, 16, 1))
    b[:, 3] = np.arange(W); w[:, 4] = 0; w[:, 5] = 63
    x[:, 5] = 255 * (rng.random((N, 16, W)) < 0.85); x[1::2, 5] = rng.integers(200, 256, (N // 2, 16, W))
    x[:, 6] |= 15; w[:, 7, :15] = 0; w[:, 7, 15] = rng.integers(1, 64, N)
    return pack(x, b, c, w)
def setup_inputs_heavy(rng):
    x, b, c, w = parts(rng); k = np.arange(16)[:, None]; q = int(rng.integers(0, N)); A = 15 * (L - 1)
    s = rng.integers(0, 16, (N, 8, 16, W)); x = np.where(np.arange(W) >= H, 255 - s, s)
    c = rng.integers(16, H, (N, 8, 16, L)) + H * (k % 2); b = rng.integers(16, H, (N, 8, 16, W)) + H * (k % 2)
    for g in range(8):
        p = rng.permutation(16); j = int(rng.integers(1, 15))
        if g % 4 < 2:
            hs = np.arange(227700, 240900); hs = hs[((37 * hs + A) & (2 * W - 1)) == (W, 2 * W - 1)[g % 4]]; h = int(rng.choice(hs))
            last = 192 + (h - 192) % 63; a = (h - last) // 63
            u = rng.permutation(np.repeat(np.arange(15), 15))[:a - 3600]
            val = np.insert(240 + np.bincount(u, minlength=15), j, last); w[q, g] = 63; w[q, g, j] = 1
        elif g % 4 == 2:
            val = rng.integers(0, 16, 16); val[j] = 255
        else:
            val = int(rng.integers(0, 256 - TH)) + rng.integers(0, TH + 1, 16)
        x[q, g][:, p] = val; c[q, g, :, 1 + PARTS * int(rng.integers(0, L // PARTS))] = p
    return pack(x, b, c, w)
def setup_inputs_ties(rng):
    x, b, c, w = parts(rng)
    for r in range(N):
        for g in range(0, 8, 2):
            o = rng.permutation(W); cl = np.zeros(W, np.int64); cl[o[W // 3:2 * (W // 3)]] = 1; cl[o[2 * (W // 3):]] = 2
            lo = int(rng.integers(0, 255 - TH)); x[r, g] = np.array([lo, lo + TH, lo + TH + 1])[cl][None, :]
            n = rng.choice(np.array([0, 1, AC - 1, AC, AC + 1, 15]), L)
            if r == 0 and g == 0: n[:] = AC
            if r == 0 and g == 2: n[:] = AC + 1
            cr = np.zeros((17, L), bool); cr[1:16] = np.argsort(np.argsort(rng.random((15, L)), axis=0), axis=0) < n
            s = 2 * ((np.add.accumulate(cr[:16].astype(np.int64), axis=0) + rng.integers(0, 2, L)) % 2)
            s = np.where(~cr[:16] & ~cr[1:] & (rng.random((16, L)) < 0.5), 1, s)
            for a in range(3):
                mem = np.flatnonzero(cl == a); c[r, g] = np.where(s == a, mem[rng.integers(0, mem.size, (16, L))], c[r, g])
    return pack(x, b, c, w)
def setup_inputs_spread(rng):
    x, b, c, w = parts(rng); lo = rng.choice(np.array([0.0, 5.0, 7.0]), (N, 8, 1, 1))
    x = np.minimum((np.exp2(lo + (8 - lo) * rng.random((N, 8, 1, W))) * rng.random((N, 8, 16, W))).astype(np.int64), 255)
    x = np.where(rng.random((N, 8, 1, W)) < 0.25, 255 - x, x)
    c = np.minimum((W * rng.random((N, 8, 16, L)) ** 3).astype(np.int64), W - 1); b = np.minimum((W * rng.random((N, 8, 16, W)) ** 2).astype(np.int64), W - 1)
    w = np.minimum(np.exp2(6 * rng.random((N, 8, 16))).astype(np.int64), 63)
    return pack(x, b, c, w)
def check_inputs(d):
    bad = []
    for k, hi in (("x", 255), ("pk", W * W - 1), ("cb", W - 1), ("wt", 63)):
        a = np.asarray(d[k]).astype(np.float64)
        if not np.all((a >= 0) & (a <= hi) & (a == np.floor(a))): bad.append("range of " + k)
    return bad
def reference(x, pk, cb, wt):
    X = x.astype(np.float32).astype(np.int64).reshape(N, 8, 16, W); p = pk.astype(np.int64).reshape(N, 8, 16, H)
    B = np.concatenate([p & (W - 1), p >> LB], axis=3)
    c = cb.astype(np.int64).reshape(N, 8, 16, L); w = wt.astype(np.int64).reshape(N, 8, 16, 1)
    lane = np.arange(L); rr = np.arange(N)[:, None, None, None]; gg = np.arange(8)[None, :, None, None]
    for t in range(T):
        e = np.take_along_axis(X, c, 3)
        z = np.concatenate([np.zeros((N, 8, 1, L), np.int64), e[:, :, :15] & 15], axis=2)
        v = X[rr, gg, z, c]
        cr = np.concatenate([np.zeros((N, 8, 1, L), bool), np.abs(v[:, :, 1:] - v[:, :, :15]) > TH], axis=2)
        n = np.add.reduce(cr.astype(np.int64), axis=2); A = np.add.reduce(n, axis=2)[:, :, None]; h = np.add.reduce(w * v, axis=2)
        ok = n <= AC; place = S * ((h + A) & (Q - 1)) + lane; nxt = (37 * h + A) & (W - 1)
        mend = np.where(cr, np.take_along_axis(B, c, 3), c)
        X, B = np.array(X), np.array(B)
        for r in range(N):
            for m in range(PARTS):
                q = r if m == 0 else (r + 1 + (t + m - 1) % (N - 1)) % N
                for g in range(8):
                    i = lane[m::PARTS]; i = i[ok[r, g, i]]
                    X[q, g][:, place[r, g, i]] = v[r, g][:, i]; B[q, g][:, place[r, g, i]] = c[r, g][:, i]
        new = np.take_along_axis(B, np.repeat(nxt[:, :, None, :], 16, axis=2), 3)
        c = np.where(ok[:, :, None, :], new, mend)
    return {"yx": X.reshape(N, 128, W).astype(np.float32).astype(BF), "yc": c.reshape(N, 128, L).astype(np.float32)}

@@ -1,0 +1,473 @@
+from concourse.mybir import AluOpType as OP, AxisListType, ActivationFunctionType as AF
+
+N, NT = 4, 4
+L, HB, W = 448, 224, 2048
+CHUNKS = [(0, 96), (96, 128), (224, 128), (352, 96)]
+MEND, BTAB = 0, 448
+BW, XW = 448 + 4096, 4096
+PLAN = {'x0': 'sxxxsxxsssssss', 'x1': 'xsxxsxsxsxvsxs', 'r0': 'xssssxssxsxxsx', 'r1': 'ssxssxssxsssvx',
+        'adj': {'BG': -16.4, 'v': -15.0, 'y': 37.1, 'XG': -6.9, 'm2': 52.0, 'XS even': -5.0, 'BS even': -34.4, 'q': 26.5,
+                'BX': -29.2, 'relu': -0.5, 't1': 13.7, 'sq': 1.0, 'U': -24.0, 'E': 9.1, 'h': -30}, 'delta': 0.02}
+
+F32, B16, I32, U16, H16 = "float32", "bfloat16", "int32", "uint16", "float16"
+SCRATCH = {}
+for _n, _w, _d in (
+        ("X", XW, B16), ("B", BW, F32), ("pki", 1024, I32), ("tlo", 1024, I32), ("thi", 1024, I32), ("cbi", L, I32), ("wti", 8, I32),
+        ("C0", L, U16), ("C1", L, U16), ("CF0", L, H16), ("CF1", L, H16), ("G", 16 * L, B16), ("GB", 16 * L, H16), ("R", 15 * L, B16),
+        ("QI", 2 * L, I32), ("FT", 2 * L, B16), ("V0", L, B16), ("V1", L, B16), ("AB", L, B16), ("SG", L, B16), ("CR", L, B16),
+        ("M2", L, H16), ("YC", L, F32), ("SUMS", 8, F32), ("SA", 8, F32), ("A1", 8, F32), ("hbf", 32, F32), ("rej", 32, F32),
+        ("acc", 32, F32), ("t1", 32, I32), ("t2", 32, I32), ("t3", 32, F32), ("n1", 32, I32), ("n2", 32, I32), ("n3", 32, F32),
+        ("n4", 32, F32), ("dl", 32, F32), ("LS0", 32, U16), ("LS1", 32, U16), ("NL", 32, U16),
+        ("COL", 144, F32), ("KC", 128, F32), ("GC", 128, F32), ("M64", 128, F32), ("PI", 8, I32), ("PF", 8, F32), ("KI", 8, I32),
+        ("GI", 8, I32), ("K8I", 8, I32), ("RGI", 8, I32), ("KF", 8, F32), ("GF", 8, F32), ("K8F", 8, F32), ("RGF", 8, F32),
+        ("CFF", 8, F32), ("CBA", 8, F32), ("BIAS", 8, F32), ("P1", 8, F32), ("K2", 8, F32), ("NEG", 8, F32), ("IB0", 32, F32),
+        ("IB", 32, F32), ("MC0", 32, F32), ("MC", 32, F32), ("RM", 16, F32), ("RM8", 8, F32), ("ID", 128, B16), ("ID16", 128, H16),
+        ("NI16", 128, H16), ("F", 144, B16), ("BA", 128, B16), ("EL", 15 * 128, B16), ("ZM", 128, B16), ("KV", 128, B16),
+        ("ZB", 128, B16), ("ZL", 8 * 128, B16), ("S16", 16 * 128, H16), ("S0", 128, B16), ("SH", 128, B16), ("KM", 128, B16),
+        ("DF0", 128, B16), ("DF", 128, B16), ("OB", 128, F32), ("WF", 8, F32), ("W4I", 8, I32), ("W4F", 8, F32), ("FW", 144, B16),
+        ("FW4", 144, B16)):
+    SCRATCH[_n] = ("sbuf", [128, _w], _d)
+for _t in range(NT):
+    SCRATCH["rc%d" % _t] = ("sbuf", [128, HB], U16)
+    SCRATCH["rv%d" % _t] = ("sbuf", [128, HB], B16)
+    SCRATCH["rl%d" % _t] = ("sbuf", [128, 16], U16)
+for _n in ("pE0", "pE1", "pU0", "pU1", "pU2", "pV", "pS", "pB"):
+    SCRATCH[_n] = ("psum", [128, 512], F32)
+SEMAPHORES = (["qv", "qs", "qt", "qg", "dcb", "dx", "dpk", "dwt", "oyx", "oyc"]
+              + [a + b + str(t) for a in "rl" for b in "CVL" for t in range(NT)])
+
+CY = 0.00083 * 1.2
+TCY = 0.00042 * 1.2
+GAM, SCA = 1.56, 3.0
+LAT = 0.1
+
+
+def R(buf, c0, c1, step=1, p0=0, p1=128):
+    return (buf, c0, c1, step, p0, p1)
+
+
+def ap(T, a):
+    buf, c0, c1, step, p0, p1 = a
+    if step == 1:
+        return T[buf][p0:p1, c0:c1]
+    return T[buf][p0:p1, c0:c1:step]
+
+
+def val(T, s):
+    return ap(T, s) if isinstance(s, tuple) else s
+
+
+def build_ops(nsig):
+    ops = []
+
+    def add(eng, fn, reads, writes, cost, tok=None, name="", after=()):
+        ops.append(dict(eng=eng, fn=fn, reads=list(reads), writes=list(writes), cost=cost, tok=tok, name=name, after=list(after)))
+        return len(ops) - 1
+
+    def ne(a):
+        return -((a[1] - a[2]) // a[3])
+
+    def vc(n):
+        return 0.06 + max(64, n) * CY
+
+    def cp(out, in_, cyc=1.0, name="copy"):
+        add("v", lambda g, T, X: g.vector.tensor_copy(ap(T, out), ap(T, in_)), [in_], [out], vc(ne(out) * cyc), name=name)
+
+    def ts(out, in0, s1, s2, op0, op1=None, cyc=1.0, name="ts"):
+        def fn(g, T, X):
+            if op1 is None:
+                return g.vector.tensor_scalar(ap(T, out), ap(T, in0), val(T, s1), None, op0)
+            return g.vector.tensor_scalar(ap(T, out), ap(T, in0), val(T, s1), val(T, s2), op0, op1)
+        add("v", fn, [in0] + [s for s in (s1, s2) if isinstance(s, tuple)], [out], vc(ne(out) * cyc), name=name)
+
+    def tt(out, a, b, op, cyc=2.0, name="tt"):
+        add("v", lambda g, T, X: g.vector.tensor_tensor(ap(T, out), ap(T, a), ap(T, b), op), [a, b], [out], vc(ne(out) * cyc), name=name)
+
+    def ms(out, x):
+        add("v", lambda g, T, X: g.vector.memset(ap(T, out), x), [], [out], vc(ne(out)), name="memset")
+
+    def act(out, in_, func, bias=0.0, scale=1.0, accum=None, name="act"):
+        def fn(g, T, X):
+            if accum is None:
+                return g.scalar.activation(ap(T, out), ap(T, in_), func, bias=val(T, bias), scale=val(T, scale))
+            return g.scalar.activation(ap(T, out), ap(T, in_), func, bias=val(T, bias), scale=val(T, scale), accum_out=ap(T, accum))
+        add("s", fn, [in_] + [s for s in (bias, scale) if isinstance(s, tuple)], [out] + ([accum] if accum else []), 0.08 + ne(out) * CY, name=name)
+
+    def gat(eng, out, win, off, name):
+        def fv(g, T, X):
+            return g.vector.tensor_copy(ap(T, out), ap(T, win).indirect(ap(T, off)))
+
+        def fs(g, T, X):
+            return g.scalar.activation(ap(T, out), ap(T, win).indirect(ap(T, off)), AF.Copy)
+        add(eng, {"v": fv, "s": fs}, [win, off], [out], 0.06 + ne(out) * GAM * CY, name=name)
+
+    def sca(win, off, in_, name):
+        add("v", lambda g, T, X: g.vector.tensor_copy(ap(T, win).indirect(ap(T, off)), ap(T, in_)), [in_, off], [win],
+            0.06 + ne(in_) * SCA * CY, name=name)
+
+    def mm(lst, name, f32=False):
+        def fn(g, T, X):
+            i = None
+            for o, l, r, a, b in lst:
+                i = g.tensor.matmul(ap(T, o), ap(T, l), ap(T, r), a, b)
+            return i
+        cost = sum(max(64, ne(r)) for _o, _l, r, _a, _b in lst) * TCY * (4 if f32 else 1)
+        add("t", fn, [x for m in lst for x in (m[1], m[2])], [m[0] for m in lst], 0.05 + cost, name=name)
+
+    def iota(out, pat, base, cm, f32=True):
+        def fn(g, T, X):
+            if f32:
+                return g.iota(ap(T, out), pat, base, cm, allow_small_or_imprecise_dtypes=True)
+            return g.iota(ap(T, out), pat, base, cm)
+        add("g", fn, [], [out], 0.15 + 2 * ne(out) * CY, name="iota")
+
+    def c1(b):
+        return R(b, 0, 1)
+
+    def whole(b):
+        return R(b, 0, SCRATCH[b][1][1])
+
+    def scaled(o, base, col, name):
+        def fv(g, T, X):
+            return g.vector.tensor_scalar(ap(T, o), ap(T, base), ap(T, col), None, OP.mult)
+
+        def fs(g, T, X):
+            return g.scalar.activation(ap(T, o), ap(T, base), AF.Copy, scale=ap(T, col))
+        add("vs", {"v": fv, "s": fs}, [base, col], [o], 0.12, name=name)
+
+    add("y", lambda g, T, X: g.sync.dma_start(T.cbi[:, :], T.cb[:, :]), [], [R("cbi", 0, L)], 2.5, ("dcb", 16), "ld cb")
+    add("sd", lambda g, T, X: g.scalar.dma_start(T.X[:, 0:W], T.x[:, :]), [], [R("X", 0, W)], 4.5, ("dx", 16), "ld x")
+    add("y", lambda g, T, X: g.sync.dma_start(T.wti[:, 0:1], T.wt[:, :]), [], [c1("wti")], 2.0, ("dwt", 16), "ld wt")
+    add("y", lambda g, T, X: g.sync.dma_start(T.pki[:, :], T.pk[:, :]), [], [R("pki", 0, 1024)], 4.5, ("dpk", 16), "ld pk")
+    iota(c1("PI"), [[1, 1]], 0, 1, False)
+    iota(c1("PF"), [[1, 1]], 0, 1)
+    iota(R("M64", 0, 128), [[0, 2], [1, 64]], 0, 0)
+    iota(R("COL", 0, 144), [[1, 144]], 0, 0)
+    iota(R("GC", 0, 128), [[1, 8], [0, 16]], 0, 0)
+    iota(R("KC", 0, 128), [[0, 8], [1, 16]], 0, 0)
+    iota(R("IB0", 0, 14), [[32, 14]], 1, 0)
+    iota(R("IB0", 14, 28), [[32, 14]], 0, 0)
+    iota(R("MC0", 0, 28), [[16, 28]], -448, 0)
+    ts(c1("KI"), c1("PI"), 15, None, OP.bitwise_and)
+    ts(c1("GI"), c1("PI"), 4, None, OP.logical_shift_right)
+    ts(c1("K8I"), c1("PI"), 7, None, OP.bitwise_and)
+    ts(c1("RGI"), c1("PI"), 63, 3, OP.bitwise_and, OP.logical_shift_right)
+    cp(c1("KF"), c1("KI"))
+    cp(c1("GF"), c1("GI"))
+    cp(c1("K8F"), c1("K8I"))
+    cp(c1("RGF"), c1("RGI"))
+    cp(R("C0", 0, HB), R("cbi", 1, L, 2), name="c16")
+    cp(R("C0", HB, L), R("cbi", 0, L, 2), name="c16")
+    ts(c1("CBA"), c1("GF"), 8.0, c1("K8F"), OP.mult, OP.add)
+    ts(whole("BA"), whole("M64"), c1("CBA"), 0.0625, OP.is_equal, OP.mult)
+    ts(R("RM", 0, 16), R("COL", 0, 16), c1("KF"), None, OP.is_equal)
+    for k in range(15):
+        scaled(R("EL", 128 * k, 128 * k + 128), whole("BA"), R("RM", k, k + 1), "EL")
+    ts(whole("ID"), R("COL", 0, 128), c1("PF"), None, OP.is_equal)
+    ts(R("RM8", 0, 8), R("COL", 0, 8), c1("K8F"), None, OP.is_equal)
+    ts(whole("ZM"), whole("GC"), c1("RGF"), None, OP.is_equal)
+    ts(R("KV", 0, 128, 1, 0, 64), R("KC", 0, 128, 1, 0, 64), 8192.0, None, OP.mult)
+    ms(R("KV", 0, 128, 1, 64, 128), -65536.0)
+    tt(whole("ZB"), whole("ZM"), whole("KV"), OP.mult)
+    for s in range(8):
+        scaled(R("ZL", 128 * s, 128 * s + 128), whole("ZB"), R("RM8", s, s + 1), "ZL")
+    ts(c1("K2"), c1("KF"), -256.0, None, OP.mult)
+    tt(c1("BIAS"), c1("KF"), c1("K2"), OP.mult)
+    ts(c1("CFF"), c1("GF"), 16.0, 15.0, OP.mult, OP.add)
+    ts(whole("F"), whole("COL"), c1("CFF"), None, OP.is_equal)
+    ts(whole("S0"), whole("ID"), R("RM", 0, 1), None, OP.mult)
+    ts(c1("P1"), c1("PF"), 1.0, None, OP.add)
+    ts(whole("SH"), R("COL", 0, 128), c1("P1"), None, OP.is_equal)
+    tt(whole("DF0"), whole("ID"), whole("SH"), OP.subtract)
+    ts(whole("KM"), whole("KC"), 0.0, None, OP.is_gt)
+    tt(whole("DF"), whole("DF0"), whole("KM"), OP.mult)
+    ms(c1("NEG"), -80.5)
+    cp(c1("WF"), c1("wti"))
+    ts(c1("W4I"), c1("wti"), 3, None, OP.bitwise_and)
+    cp(c1("W4F"), c1("W4I"))
+    ts(whole("FW4"), whole("F"), c1("W4F"), 512.0, OP.mult, OP.mult)
+    ts(whole("FW"), whole("F"), c1("WF"), None, OP.mult)
+    ts(whole("OB"), whole("GC"), c1("GF"), 256.0, OP.is_equal, OP.mult)
+    ts(c1("K2"), c1("KF"), 2.0, None, OP.mult)
+    ts(R("IB", 0, 28), R("IB0", 0, 28), c1("K2"), None, OP.add)
+    ts(R("MC", 0, 28), R("MC0", 0, 28), c1("KF"), 1.0 / 2048, OP.add, OP.mult)
+    ts(whole("ID16"), R("COL", 0, 128), c1("PF"), None, OP.is_equal)
+    ts(whole("NI16"), whole("ID16"), -1.0, None, OP.mult)
+    for k in range(1, 16):
+        ts(R("S16", 128 * k, 128 * k + 128), whole("ID16"), R("RM", k, k + 1), None, OP.mult, cyc=0.5, name="S16")
+    ts(whole("tlo"), whole("pki"), W - 1, None, OP.bitwise_and)
+    cp(R("B", BTAB, BTAB + 1024), whole("tlo"))
+    ts(whole("thi"), whole("pki"), 11, None, OP.logical_shift_right)
+    cp(R("B", BTAB + 1024, BTAB + 2048), whole("thi"))
+    cp(whole("CF0"), whole("C0"), 0.5)
+
+    xw, bw = R("X", 0, W), R("B", BTAB, BTAB + W)
+    ub, un = ["pU0", "pU1", "pU2"], 0
+    nc = len(CHUNKS)
+
+    for t in range(NT):
+        C, CF, V, LS = "C%d" % (t % 2), "CF%d" % (t % 2), "V%d" % (t % 2), "LS%d" % (t % 2)
+
+        def send(what, src, dst, t=t):
+            def fn(g, T, X):
+                rid, pid, m = X[t]
+                return g.remote_dma(ap(T, dst), ap(T, src), T.sem["r%s%d" % (what, t)], T.sem["l%s%d" % (what, t)], pid, rid, m)
+            i = add("g", fn, [src], [], 0.6, ("l%s%d" % (what, t), nsig), "send " + what)
+            add("x", None, [], [dst], 2.2, ("r%s%d" % (what, t), nsig), "recv " + what, [i])
+
+        send("C", R(C, 0, HB), R("rc%d" % t, 0, HB))
+        for c, (i0, n) in enumerate(CHUNKS):
+            i1, g0 = i0 + n, 16 * i0
+            for j in range(i0, i1, 32):
+                gat("vs", R("G", 16 * j, 16 * j + 512), xw, R(C, j, j + 32), "XG")
+            pe = "pE%d" % (c % 2)
+            mm([(R(pe, (k // 8) * n, (k // 8) * n + n), R("EL", 128 * k, 128 * k + 128), R("G", g0 + k, 16 * i1, 16),
+                 k % 8 == 0, k in (7, 14)) for k in range(15)], "E")
+            q, f = R("QI", 2 * i0, 2 * i1), R("FT", 2 * i0, 2 * i1)
+            ts(q, R(pe, 0, 2 * n), 0.46875, None, OP.subtract, name="q")
+            tt(f, R(pe, 0, 2 * n), q, OP.subtract, 1.0, name="y")
+            fl = R("FT", 2 * i0, 2 * i1, 1, 64, 128)
+            act(fl, fl, AF.Square, name="sq")
+            mm([(R("pV", 0, n), whole("S0"), R("G", g0, 16 * i1, 16), True, False)], "v0")
+            per = 512 // n
+            for b in range(0, 15, per):
+                kk = list(range(1, 16))[b:b + per]
+                u = ub[un % 3]
+                un += 1
+                lst = []
+                for x, k in enumerate(kk):
+                    o, s, h = R(u, x * n, x * n + n), (k - 1) % 8, (k - 1) // 8
+                    lst.append((o, whole("ID"), R("G", g0 + k, 16 * i1, 16), True, False))
+                    lst.append((o, R("ZL", 128 * s, 128 * s + 128), R("FT", 2 * i0 + h * n, 2 * i0 + h * n + n), False, True))
+                mm(lst, "U")
+                r0 = 15 * i0 + b * n
+                ro, ui = R("R", r0, r0 + len(kk) * n), R(u, 0, len(kk) * n)
+
+                def fv(g, T, X, ro=ro, ui=ui):
+                    return g.vector.tensor_scalar(ap(T, ro), ap(T, ui), T.BIAS[:, 0:1], 0.0, OP.add, OP.max)
+
+                def fs(g, T, X, ro=ro, ui=ui):
+                    return g.scalar.activation(ap(T, ro), ap(T, ui), AF.Relu, bias=T.BIAS[:, 0:1])
+                add("vs", {"v": fv, "s": fs}, [ui, c1("BIAS")], [ro], 0.08 + len(kk) * n * CY, name="relu")
+                mm([(R("pV", 0, n), R("F", 15 - k, 143 - k), R("R", 15 * i0 + (k - 1) * n, 15 * i0 + k * n), False, k == 15) for k in kk], "v")
+            vv = R(V, i0, i1)
+            act(vv, R("pV", 0, n), AF.Copy, name="vcopy")
+            mm([(R("pS", 0, n), whole("DF"), vv, True, True)], "d")
+            act(R("AB", i0, i1), R("pS", 0, n), AF.Abs, name="abs")
+            act(R("SG", i0, i1), R("AB", i0, i1), AF.Sign, bias=c1("NEG"), accum=R("SUMS", c, c + 1), name="sign")
+            ts(R("CR", i0, i1), R("AB", i0, i1), 80.0, None, OP.is_gt, cyc=0.5, name="cr")
+            if i1 == HB:
+                send("V", R(V, 0, HB), R("rv%d" % t, 0, HB))
+        for c, (i0, n) in enumerate(CHUNKS):
+            i1, g0 = i0 + n, 16 * i0
+            for j in range(i0, i1, 32):
+                gat("v", R("GB", 16 * j, 16 * j + 512), bw, R(C, j, j + 32), "BG")
+            bl = ([(R("pB", 0, n), R("S16", 128 * k, 128 * k + 128), R("GB", g0 + k, 16 * i1, 16), k == 1, False) for k in range(1, 16)]
+                  + [(R("pB", 0, n), whole("NI16"), R(CF, i0, i1), False, True)])
+            for j in range(0, 16, 4):
+                mm(bl[j:j + 4], "BX")
+            tt(R("M2", i0, i1), R("pB", 0, n), R("CR", i0, i1), OP.mult, 1.0, name="m2")
+            mm([(R("pB", 256, 256 + n), whole("ID16"), R("M2", i0, i1), True, False),
+                (R("pB", 256, 256 + n), whole("ID16"), R(CF, i0, i1), False, True)], "mend")
+            act(R("B", MEND + i0, MEND + i1), R("pB", 256, 256 + n), AF.Copy, name="mend")
+
+        def wrap(bank, lh, src, name):
+            mm([(R(bank, 0, 28), R(lh, 15 - b, 143 - b), R(src, b, L, 16), b == 0, b == 15) for b in range(16)], name)
+        wrap("pU0", "FW4", V, "h4")
+        tt(R("hbf", 0, 28), R("pU0", 0, 28), R("IB", 0, 28), OP.add, 1.0, name="hb")
+        sa, su, sl = c1("SA"), R("SUMS", 0, nc - 1), R("SUMS", nc - 1, nc)
+        add("v", lambda g, T, X, sa=sa, su=su: g.vector.tensor_reduce(ap(T, sa), ap(T, su), AxisListType.X, OP.add), [su], [sa], vc(4), name="SA")
+        mm([(R("pU2", 0, 1), whole("OB"), sa, True, False), (R("pU2", 0, 1), whole("OB"), sl, False, True)], "A", True)
+        wrap("pU1", "F", "SG", "n")
+        ts(R("rej", 0, 28), R("pU1", 0, 28), -5.0, 2048.0, OP.is_gt, OP.mult, name="rej")
+        ts(R("acc", 0, 28), R("pU1", 0, 28), -5.0, None, OP.is_lt, name="acc")
+        ts(R("t1", 0, 28), R("hbf", 0, 28), R("pU2", 0, 1), None, OP.add, name="t1")
+        ts(R("t2", 0, 28), R("t1", 0, 28), 2047, None, OP.bitwise_and, name="t2")
+        tt(R("t3", 0, 28), R("t2", 0, 28), R("rej", 0, 28), OP.add, name="t3")
+        cp(R(LS, 0, 28), R("t3", 0, 28), name="list")
+        send("L", R(LS, 0, 14), R("rl%d" % t, 0, 14))
+        ts(c1("A1"), R("pU2", 0, 1), 1.0 / 512, 1536.0, OP.mult, OP.add, name="A1")
+        wrap("pE0", "FW", V, "h")
+        ts(R("n1", 0, 28), R("pE0", 0, 28), 37.0, c1("A1"), OP.mult, OP.add, name="n1")
+        ts(R("n2", 0, 28), R("n1", 0, 28), 2047, None, OP.bitwise_and, name="n2")
+        tt(R("n3", 0, 28), R("n2", 0, 28), R("acc", 0, 28), OP.mult, name="n3")
+        tt(R("dl", 0, 28), R("rej", 0, 28), R("MC", 0, 28), OP.mult, name="dl")
+        tt(R("n4", 0, 28), R("n3", 0, 28), R("dl", 0, 28), OP.add, name="n4")
+        ts(R("NL", 0, 28), R("n4", 0, 28), 448.0, None, OP.add, name="NL")
+        xs, bs = R("X", 0, XW), R("B", BTAB, BW)
+        ls, rl = R(LS, 14, 28), R("rl%d" % t, 0, 14)
+        sca(xs, ls, R(V, HB, L), "XS even")
+        sca(bs, ls, R(C, HB, L), "BS even")
+        last = t == NT - 1
+        rest = [(xs, R("rv%d" % t, 0, HB), "XS odd"), (bs, R("rc%d" % t, 0, HB), "BS odd")]
+        for w, s, nm in (rest if last else rest[::-1]):
+            sca(w, rl, s, nm)
+        bn = R("B", 0, BTAB + W)
+        if last:
+            add("y", lambda g, T, X: g.sync.dma_start(T.yx[:, :], T.X[:, 0:W]), [R("X", 0, W)], [], 4.0, ("oyx", 16), "st x")
+            gat("v", R("YC", 1, L, 2), bn, R("NL", 0, 14), "nxt")
+            gat("s", R("YC", 0, L, 2), bn, R("NL", 14, 28), "nxt")
+            add("y", lambda g, T, X: g.sync.dma_start(T.yc[:, :], T.YC[:, :]), [R("YC", 0, L)], [], 2.5, ("oyc", 16), "st c")
+        else:
+            D, DF_ = "C%d" % ((t + 1) % 2), "CF%d" % ((t + 1) % 2)
+            gat("v", R(D, 0, HB), bn, R("NL", 0, 14), "nxt")
+            gat("v", R(D, HB, L), bn, R("NL", 14, 28), "nxt")
+            cp(whole(DF_), whole(D), 0.5, name="cf")
+    return ops
+
+
+def hit(a, b):
+    return a[0] == b[0] and a[1] < b[2] and b[1] < a[2] and a[4] < b[5] and b[4] < a[5]
+
+
+def depend(ops):
+    hist, deps = {}, []
+    for i, o in enumerate(ops):
+        d = {a: True for a in o["after"]}
+        acc = [(r, False) for r in o["reads"]] + [(w, True) for w in o["writes"]]
+        for r, wr in acc:
+            ps = SCRATCH[r[0]][0] == "psum"
+            for j, q, qw in hist.get(r[0], []):
+                if j == i:
+                    continue
+                same = ops[j]["eng"] == o["eng"] and o["eng"] in ("t", "v", "s", "g")
+                over = hit(r, q) and (wr or qw)
+                if same and o["eng"] == "t":
+                    if over:
+                        d[j] = d.get(j, False)
+                elif over or (ps and not same):
+                    d[j] = True
+        deps.append(d)
+        for r, wr in acc:
+            h = hist.setdefault(r[0], [])
+            if wr and SCRATCH[r[0]][0] != "psum" and r[3] == 1:
+                h[:] = [e for e in h if e[0] == i or not (e[1][1] >= r[1] and e[1][2] <= r[2] and e[1][4] >= r[4] and e[1][5] <= r[5])]
+            h.append((i, r, wr))
+            if SCRATCH[r[0]][0] == "psum":
+                del h[:-80]
+    return deps
+
+
+def force(ops):
+    f, k = {}, {"XG": 0, "relu": 0}
+    tot = {z: sum(o["name"] == z for o in ops) // NT for z in k}
+    for i, o in enumerate(ops):
+        z = o["name"]
+        if z in k:
+            f[i] = PLAN[("x" if z == "XG" else "r") + ("0" if k[z] < tot[z] else "1")][k[z] % tot[z]]
+            k[z] += 1
+    return {i: ("vs" if v == "x" else v) for i, v in f.items()}
+
+
+def schedule(ops, deps):
+    n = len(ops)
+    fc, adj, delta = force(ops), PLAN["adj"], PLAN["delta"]
+    succ = [[] for _ in range(n)]
+    for i in range(n):
+        for j in deps[i]:
+            succ[j].append(i)
+    pri = [0.0] * n
+    for i in range(n - 1, -1, -1):
+        pri[i] = ops[i]["cost"] + max([pri[s] + LAT for s in succ[i]] or [0.0])
+    pri = [pri[i] + adj.get(ops[i]["name"], 0.0) for i in range(n)]
+    left = [len(d) for d in deps]
+    ready = {i: 0.0 for i in range(n) if left[i] == 0}
+    free = {"v": 0.0, "s": 0.0, "t": 0.0, "g": 0.0, "y": 0.0}
+    fin, order = [0.0] * n, []
+    while ready:
+        best, heads = None, {}
+        for i, r in ready.items():
+            e = ops[i]["eng"]
+            if e == "x":
+                best = (r, "x", i)
+                break
+            if e == "vs":
+                e = fc.get(i, "vs")
+            for q in ("v", "s") if e == "vs" else (("s",) if e == "sd" else (e,)):
+                heads.setdefault(q, []).append((max(free[q], r), i))
+        if best is None:
+            for q, c in heads.items():
+                t0 = min(c)[0]
+                st, i = max(c, key=lambda z: (z[0] <= t0 + delta, pri[z[1]], -z[1]))
+                if best is None or st < best[0]:
+                    best = (st, q, i)
+        st, q, i = best
+        del ready[i]
+        o = ops[i]
+        if q == "x":
+            fin[i] = st + o["cost"]
+        elif o["eng"] in ("y", "sd"):
+            free[q] = st + 0.1
+            fin[i] = st + o["cost"]
+        else:
+            free[q] = fin[i] = st + o["cost"]
+        order.append((i, q))
+        for s in succ[i]:
+            left[s] -= 1
+            if left[s] == 0:
+                ready[s] = max(fin[j] + (LAT if deps[s][j] else 0.0) for j in deps[s])
+    return order, max(fin)
+
+
+_plan = {}
+
+
+def plan(nsig):
+    if nsig in _plan:
+        return _plan[nsig]
+    ops = build_ops(nsig)
+    deps = depend(ops)
+    order, span = schedule(ops, deps)
+    sem = {"v": "qv", "s": "qs", "t": "qt", "g": "qg"}
+    cnt, known, tok, snap, out = {}, {q: {} for q in "vstgy"}, {}, {}, []
+    for i, q in order:
+        o = ops[i]
+        if q == "x":
+            tok[i] = o["tok"]
+            cnt[o["tok"][0]] = o["tok"][1]
+            snap[i] = {o["tok"][0]: o["tok"][1]}
+            continue
+        kn, top = known[q], {}
+        for j in sorted((j for j, w in deps[i].items() if w), reverse=True):
+            s, v = tok[j]
+            if kn.get(s, 0) < v:
+                top[s] = max(top.get(s, 0), v)
+                for a, b in snap[j].items():
+                    if kn.get(a, 0) < b:
+                        kn[a] = b
+        if o["tok"]:
+            tok[i] = o["tok"]
+            cnt[o["tok"][0]] = o["tok"][1]
+        else:
+            s = sem[q]
+            cnt[s] = cnt.get(s, 0) + 1
+            tok[i] = (s, cnt[s])
+        snap[i] = dict(kn)
+        snap[i][tok[i][0]] = tok[i][1]
+        out.append((q, o, sorted(top.items()), tok[i]))
+    _plan[nsig] = (out, cnt, span)
+    return _plan[nsig]
+
+
+def rank_program(g, core, T, topo):
+    rank = T.rank_of(core)
+    if rank is None:
+        return
+    X = []
+    for t in range(NT):
+        d = T.cores[(rank + 1 + t % (N - 1)) % N]
+        rid, pid = topo.addr(d, core)
+        X.append((rid, pid, topo.mask(core, d)))
+    out, cnt, _span = plan(len(topo.engines(core, T.cores[(rank + 1) % N])))
+    queue = {"v": g.vector, "s": g.scalar, "t": g.tensor, "g": g, "y": g.sync}
+    for q, o, waits, tk in out:
+        for s, v in waits:
+            queue[q].wait_ge(T.sem[s], v)
+        fn = o["fn"][q] if isinstance(o["fn"], dict) else o["fn"]
+        ins = fn(g, T, X)
+        if o["tok"] is None:
+            ins.then_inc(T.sem[tk[0]], 1)
+        elif o["name"][:4] != "send":
+            ins.then_inc(T.sem[tk[0]], tk[1])
+    for s, v in sorted(cnt.items()):
+        g.wait_ge(T.sem[s], v)

@@ -3,29 +3,33 @@ from concourse.mybir import AluOpType as OP, AxisListType, ActivationFunctionTyp
 N, NT = 4, 4
 L, HB, W = 448, 224, 2048
 CHUNKS = [(0, 96), (96, 128), (224, 128), (352, 96)]
+PIECE = 64
 MEND, BTAB = 0, 448
 BW, XW = 448 + 4096, 4096
-PLAN = {'x0': 'sxxxsxxsssssss', 'x1': 'xsxxsxsxsxvsxs', 'r0': 'xssssxssxsxxsx', 'r1': 'ssxssxssxsssvx',
-        'adj': {'BG': -16.4, 'v': -15.0, 'y': 37.1, 'XG': -6.9, 'm2': 52.0, 'XS even': -5.0, 'BS even': -34.4, 'q': 26.5,
-                'BX': -29.2, 'relu': -0.5, 't1': 13.7, 'sq': 1.0, 'U': -24.0, 'E': 9.1, 'h': -30}, 'delta': 0.02}
+PLAN = {'x0': 'xsxxxxsx', 'x1': 'svvsxvss', 'r0': 'sssvssssxxssxs', 'r1': 'vxsssxsxssxxxs',
+        'adj': {'BG': -31.6, 'v': -16.3, 'XG': -14.6, 'm2': 68.5, 'BX': -100.8, 'relu': 7.5, 'U': -34.2, 'E': 49.3, 'v0': 42.2,
+                'abs': -28.5, 'copy': 7.2, 'A': 9.5, 'ZL': 17.7, 'relu@1': -14.9, 'd': 16.1, 'sign@1': -10.3, 'EL': -11.1,
+                'v@1': 33.3, 'S16': 10.7, 'rej': -17.6, 'v@0': 10.2, 'abs@2': 35.9, 't2': -21.6, 'relu@2': 7.5, 'BX@2': -6.0,
+                'BG@3': -27.0, 'BX@1': -6.5}, 'delta': 0.06, 'wf': 0.11}
 
 F32, B16, I32, U16, H16 = "float32", "bfloat16", "int32", "uint16", "float16"
 SCRATCH = {}
 for _n, _w, _d in (
         ("X", XW, B16), ("B", BW, F32), ("pki", 1024, I32), ("tlo", 1024, I32), ("thi", 1024, I32), ("cbi", L, I32), ("wti", 8, I32),
         ("C0", L, U16), ("C1", L, U16), ("CF0", L, H16), ("CF1", L, H16), ("G", 16 * L, B16), ("GB", 16 * L, H16), ("R", 15 * L, B16),
-        ("QI", 2 * L, I32), ("FT", 2 * L, B16), ("V0", L, B16), ("V1", L, B16), ("AB", L, B16), ("SG", L, B16), ("CR", L, B16),
-        ("M2", L, H16), ("YC", L, F32), ("SUMS", 8, F32), ("SA", 8, F32), ("A1", 8, F32), ("hbf", 32, F32), ("rej", 32, F32),
-        ("acc", 32, F32), ("t1", 32, I32), ("t2", 32, I32), ("t3", 32, F32), ("n1", 32, I32), ("n2", 32, I32), ("n3", 32, F32),
-        ("n4", 32, F32), ("dl", 32, F32), ("LS0", 32, U16), ("LS1", 32, U16), ("NL", 32, U16),
-        ("COL", 144, F32), ("KC", 128, F32), ("GC", 128, F32), ("M64", 128, F32), ("PI", 8, I32), ("PF", 8, F32), ("KI", 8, I32),
-        ("GI", 8, I32), ("K8I", 8, I32), ("RGI", 8, I32), ("KF", 8, F32), ("GF", 8, F32), ("K8F", 8, F32), ("RGF", 8, F32),
-        ("CFF", 8, F32), ("CBA", 8, F32), ("BIAS", 8, F32), ("P1", 8, F32), ("K2", 8, F32), ("NEG", 8, F32), ("IB0", 32, F32),
-        ("IB", 32, F32), ("MC0", 32, F32), ("MC", 32, F32), ("RM", 16, F32), ("RM8", 8, F32), ("ID", 128, B16), ("ID16", 128, H16),
-        ("NI16", 128, H16), ("F", 144, B16), ("BA", 128, B16), ("EL", 15 * 128, B16), ("ZM", 128, B16), ("KV", 128, B16),
-        ("ZB", 128, B16), ("ZL", 8 * 128, B16), ("S16", 16 * 128, H16), ("S0", 128, B16), ("SH", 128, B16), ("KM", 128, B16),
-        ("DF0", 128, B16), ("DF", 128, B16), ("OB", 128, F32), ("WF", 8, F32), ("W4I", 8, I32), ("W4F", 8, F32), ("FW", 144, B16),
-        ("FW4", 144, B16)):
+        ("QI", L, I32), ("Y", L, B16), ("FT", 2 * L, B16), ("V0", L, B16), ("V1", L, B16), ("AB", L, B16), ("SG", L, B16),
+        ("CR", L, B16), ("VT", 8 * 128, B16), ("M2", L, H16), ("YC", L, F32), ("SUMS", 8, F32), ("SA", 8, F32), ("hbf", 32, F32),
+        ("rej", 32, F32), ("acc", 32, F32), ("t1", 32, I32), ("t2", 32, I32), ("t3", 32, F32), ("n1", 32, I32), ("n5", 32, I32),
+        ("n6", 32, I32), ("n2", 32, I32), ("n3", 32, F32), ("n4", 32, F32), ("dl", 32, F32), ("LS0", 32, U16), ("LS1", 32, U16),
+        ("NL", 32, U16), ("COL", 144, F32), ("KC", 128, F32), ("GC", 128, F32), ("M64", 128, F32), ("PI", 8, I32), ("PF", 8, F32),
+        ("KI", 8, I32), ("GI", 8, I32), ("K8I", 8, I32), ("RGI", 8, I32), ("KF", 8, F32), ("GF", 8, F32), ("K8F", 8, F32),
+        ("RGF", 8, F32), ("CFF", 8, F32), ("CBA", 8, F32), ("BIAS", 8, F32), ("P1", 8, F32), ("K2", 8, F32), ("NEG", 8, F32),
+        ("ONE", 8, F32), ("HALF", 8, F32), ("KD", 8, F32), ("KLO", 8, F32), ("IB0", 32, F32), ("IB", 32, F32), ("MC0", 32, F32),
+        ("MC", 32, F32), ("RM", 16, F32), ("RM8", 8, F32), ("ID", 128, B16), ("ID6", 128, B16), ("ID16", 128, H16),
+        ("NI16", 128, H16), ("F", 144, B16), ("BA", 128, B16), ("DA", 128, B16), ("DB", 128, B16), ("EL", 15 * 128, B16),
+        ("ZM", 128, B16), ("KV", 128, B16), ("ZB", 128, B16), ("ZL", 8 * 128, B16), ("S16", 16 * 128, H16), ("O8", 8, B16),
+        ("O80", 8, B16), ("SH", 128, B16), ("KM", 128, B16), ("DF0", 128, B16), ("DF", 128, B16), ("OB", 128, F32), ("WF", 8, F32),
+        ("FW", 144, B16)):
     SCRATCH[_n] = ("sbuf", [128, _w], _d)
 for _t in range(NT):
     SCRATCH["rc%d" % _t] = ("sbuf", [128, HB], U16)
@@ -36,10 +40,7 @@ for _n in ("pE0", "pE1", "pU0", "pU1", "pU2", "pV", "pS", "pB"):
 SEMAPHORES = (["qv", "qs", "qt", "qg", "dcb", "dx", "dpk", "dwt", "oyx", "oyc"]
               + [a + b + str(t) for a in "rl" for b in "CVL" for t in range(NT)])
 
-CY = 0.00083 * 1.2
-TCY = 0.00042 * 1.2
-GAM, SCA = 1.56, 3.0
-LAT = 0.1
+CY, TCY, GAM, SCA, LAT = 0.00083 * 1.15, 0.00042 * 1.15, 1.4, 3, 0.1
 
 
 def R(buf, c0, c1, step=1, p0=0, p1=128):
@@ -58,10 +59,10 @@ def val(T, s):
 
 
 def build_ops(nsig):
-    ops = []
+    ops, ck = [], [9]
 
     def add(eng, fn, reads, writes, cost, tok=None, name="", after=()):
-        ops.append(dict(eng=eng, fn=fn, reads=list(reads), writes=list(writes), cost=cost, tok=tok, name=name, after=list(after)))
+        ops.append(dict(eng=eng, fn=fn, reads=list(reads), writes=list(writes), cost=cost, tok=tok, name=name, after=list(after), ck=ck[0]))
         return len(ops) - 1
 
     def ne(a):
@@ -159,37 +160,44 @@ def build_ops(nsig):
     cp(R("C0", 0, HB), R("cbi", 1, L, 2), name="c16")
     cp(R("C0", HB, L), R("cbi", 0, L, 2), name="c16")
     ts(c1("CBA"), c1("GF"), 8.0, c1("K8F"), OP.mult, OP.add)
-    ts(whole("BA"), whole("M64"), c1("CBA"), 0.0625, OP.is_equal, OP.mult)
+    ts(whole("ID6"), R("COL", 0, 128), c1("PF"), 0.0625, OP.is_equal, OP.mult)
+    ts(whole("BA"), whole("M64"), c1("CBA"), None, OP.is_equal)
     ts(R("RM", 0, 16), R("COL", 0, 16), c1("KF"), None, OP.is_equal)
     for k in range(15):
-        scaled(R("EL", 128 * k, 128 * k + 128), whole("BA"), R("RM", k, k + 1), "EL")
+        scaled(R("EL", 128 * k, 128 * k + 128), whole("ID6"), R("RM", k, k + 1), "EL")
     ts(whole("ID"), R("COL", 0, 128), c1("PF"), None, OP.is_equal)
+    ts(c1("KLO"), c1("KF"), 7.5, None, OP.is_lt)
+    ts(c1("KD"), c1("KF"), 7.5, None, OP.is_gt)
+    scaled(whole("DA"), whole("BA"), c1("KLO"), "DA")
+    scaled(whole("DB"), whole("BA"), c1("KD"), "DA")
+    ms(R("HALF", 0, 1, 1, 0, 64), 0.0)
+    ms(R("HALF", 0, 1, 1, 64, 128), -0.5)
     ts(R("RM8", 0, 8), R("COL", 0, 8), c1("K8F"), None, OP.is_equal)
     ts(whole("ZM"), whole("GC"), c1("RGF"), None, OP.is_equal)
-    ts(R("KV", 0, 128, 1, 0, 64), R("KC", 0, 128, 1, 0, 64), 8192.0, None, OP.mult)
-    ms(R("KV", 0, 128, 1, 64, 128), -65536.0)
+    ts(R("KV", 0, 128, 1, 0, 64), R("KC", 0, 128, 1, 0, 64), 8192.0, -65536.0, OP.mult, OP.add)
+    ts(R("KV", 0, 128, 1, 64, 128), R("KC", 0, 128, 1, 64, 128), -8192.0, None, OP.mult)
     tt(whole("ZB"), whole("ZM"), whole("KV"), OP.mult)
     for s in range(8):
         scaled(R("ZL", 128 * s, 128 * s + 128), whole("ZB"), R("RM8", s, s + 1), "ZL")
-    ts(c1("K2"), c1("KF"), -256.0, None, OP.mult)
+    ts(c1("K2"), c1("KF"), -256.0, 2048.0, OP.mult, OP.add)
     tt(c1("BIAS"), c1("KF"), c1("K2"), OP.mult)
     ts(c1("CFF"), c1("GF"), 16.0, 15.0, OP.mult, OP.add)
     ts(whole("F"), whole("COL"), c1("CFF"), None, OP.is_equal)
-    ts(whole("S0"), whole("ID"), R("RM", 0, 1), None, OP.mult)
+    ts(R("O8", 0, 8), R("COL", 0, 8), c1("GF"), None, OP.is_equal)
+    ts(R("O80", 0, 8), R("O8", 0, 8), R("RM", 0, 1), None, OP.mult)
     ts(c1("P1"), c1("PF"), 1.0, None, OP.add)
     ts(whole("SH"), R("COL", 0, 128), c1("P1"), None, OP.is_equal)
     tt(whole("DF0"), whole("ID"), whole("SH"), OP.subtract)
     ts(whole("KM"), whole("KC"), 0.0, None, OP.is_gt)
     tt(whole("DF"), whole("DF0"), whole("KM"), OP.mult)
     ms(c1("NEG"), -80.5)
+    ms(c1("ONE"), 1.0)
+    ms(c1("SUMS"), 448.0)
     cp(c1("WF"), c1("wti"))
-    ts(c1("W4I"), c1("wti"), 3, None, OP.bitwise_and)
-    cp(c1("W4F"), c1("W4I"))
-    ts(whole("FW4"), whole("F"), c1("W4F"), 512.0, OP.mult, OP.mult)
-    ts(whole("FW"), whole("F"), c1("WF"), None, OP.mult)
-    ts(whole("OB"), whole("GC"), c1("GF"), 256.0, OP.is_equal, OP.mult)
+    scaled(whole("FW"), whole("F"), c1("WF"), "FW")
+    ts(whole("OB"), whole("GC"), c1("GF"), 0.5, OP.is_equal, OP.mult)
     ts(c1("K2"), c1("KF"), 2.0, None, OP.mult)
-    ts(R("IB", 0, 28), R("IB0", 0, 28), c1("K2"), None, OP.add)
+    ts(R("IB", 0, 28), R("IB0", 0, 28), c1("K2"), 1.0 / 512, OP.add, OP.mult)
     ts(R("MC", 0, 28), R("MC0", 0, 28), c1("KF"), 1.0 / 2048, OP.add, OP.mult)
     ts(whole("ID16"), R("COL", 0, 128), c1("PF"), None, OP.is_equal)
     ts(whole("NI16"), whole("ID16"), -1.0, None, OP.mult)
@@ -217,18 +225,18 @@ def build_ops(nsig):
 
         send("C", R(C, 0, HB), R("rc%d" % t, 0, HB))
         for c, (i0, n) in enumerate(CHUNKS):
-            i1, g0 = i0 + n, 16 * i0
-            for j in range(i0, i1, 32):
-                gat("vs", R("G", 16 * j, 16 * j + 512), xw, R(C, j, j + 32), "XG")
+            i1, g0, ck[0] = i0 + n, 16 * i0, c
+            for j in range(i0, i1, PIECE):
+                e = min(j + PIECE, i1)
+                gat("vs", R("G", 16 * j, 16 * e), xw, R(C, j, e), "XG")
             pe = "pE%d" % (c % 2)
-            mm([(R(pe, (k // 8) * n, (k // 8) * n + n), R("EL", 128 * k, 128 * k + 128), R("G", g0 + k, 16 * i1, 16),
-                 k % 8 == 0, k in (7, 14)) for k in range(15)], "E")
-            q, f = R("QI", 2 * i0, 2 * i1), R("FT", 2 * i0, 2 * i1)
-            ts(q, R(pe, 0, 2 * n), 0.46875, None, OP.subtract, name="q")
-            tt(f, R(pe, 0, 2 * n), q, OP.subtract, 1.0, name="y")
-            fl = R("FT", 2 * i0, 2 * i1, 1, 64, 128)
-            act(fl, fl, AF.Square, name="sq")
-            mm([(R("pV", 0, n), whole("S0"), R("G", g0, 16 * i1, 16), True, False)], "v0")
+            mm([(R(pe, 0, n), R("EL", 128 * k, 128 * k + 128), R("G", g0 + k, 16 * i1, 16), k == 0, k == 14) for k in range(15)], "E")
+            q, y = R("QI", i0, i1), R("Y", i0, i1)
+            ts(q, R(pe, 0, n), 0.46875, None, OP.subtract, name="q")
+            tt(y, R(pe, 0, n), q, OP.subtract, 1.0, name="y")
+            mm([(R(pe, 256, 256 + n), whole("DA"), y, True, True), (R(pe, 256 + n, 256 + 2 * n), whole("DB"), y, True, True)], "yy")
+            act(R("FT", 2 * i0, 2 * i1), R(pe, 256, 256 + 2 * n), AF.Square, bias=c1("HALF"), name="sq")
+            mm([(R("pV", 0, 128, 16, 0, n), R("G", g0, 16 * i1, 16), R("O80", 0, 8), True, True)], "v0")
             per = 512 // n
             for b in range(0, 15, per):
                 kk = list(range(1, 16))[b:b + per]
@@ -249,48 +257,52 @@ def build_ops(nsig):
                 def fs(g, T, X, ro=ro, ui=ui):
                     return g.scalar.activation(ap(T, ro), ap(T, ui), AF.Relu, bias=T.BIAS[:, 0:1])
                 add("vs", {"v": fv, "s": fs}, [ui, c1("BIAS")], [ro], 0.08 + len(kk) * n * CY, name="relu")
-                mm([(R("pV", 0, n), R("F", 15 - k, 143 - k), R("R", 15 * i0 + (k - 1) * n, 15 * i0 + k * n), False, k == 15) for k in kk], "v")
-            vv = R(V, i0, i1)
-            act(vv, R("pV", 0, n), AF.Copy, name="vcopy")
+                mm([(R("pV", k, 128, 16, 0, n), R("R", 15 * i0 + (k - 1) * n, 15 * i0 + k * n), R("O8", 0, 8), True, True) for k in kk], "v")
+            vv, vt = R(V, i0, i1), R("VT", 128 * c, 128 * c + 128, 1, 0, n)
+            act(vt, R("pV", 0, 128, 1, 0, n), AF.Copy, name="vt")
+            mm([(R("pS", 128, 128 + n), vt, R("ID", 0, n, 1, 0, n), True, True)], "vn")
+            act(vv, R("pS", 128, 128 + n), AF.Copy, name="vcopy")
             mm([(R("pS", 0, n), whole("DF"), vv, True, True)], "d")
             act(R("AB", i0, i1), R("pS", 0, n), AF.Abs, name="abs")
-            act(R("SG", i0, i1), R("AB", i0, i1), AF.Sign, bias=c1("NEG"), accum=R("SUMS", c, c + 1), name="sign")
-            ts(R("CR", i0, i1), R("AB", i0, i1), 80.0, None, OP.is_gt, cyc=0.5, name="cr")
+            act(R("SG", i0, i1), R("AB", i0, i1), AF.Sign, bias=c1("NEG"), accum=R("SUMS", c + 1, c + 2), name="sign")
+            act(R("CR", i0, i1), R("SG", i0, i1), AF.Relu, name="cr")
             if i1 == HB:
                 send("V", R(V, 0, HB), R("rv%d" % t, 0, HB))
         for c, (i0, n) in enumerate(CHUNKS):
-            i1, g0 = i0 + n, 16 * i0
-            for j in range(i0, i1, 32):
-                gat("v", R("GB", 16 * j, 16 * j + 512), bw, R(C, j, j + 32), "BG")
-            bl = ([(R("pB", 0, n), R("S16", 128 * k, 128 * k + 128), R("GB", g0 + k, 16 * i1, 16), k == 1, False) for k in range(1, 16)]
-                  + [(R("pB", 0, n), whole("NI16"), R(CF, i0, i1), False, True)])
+            i1, g0, ck[0], pb = i0 + n, 16 * i0, c, ("pB", "pV", "pE1", "pS")[c]
+            for j in range(i0, i1, PIECE):
+                e = min(j + PIECE, i1)
+                gat("v", R("GB", 16 * j, 16 * e), bw, R(C, j, e), "BG")
+            bl = ([(R(pb, 0, n), R("S16", 128 * k, 128 * k + 128), R("GB", g0 + k, 16 * i1, 16), k == 1, False) for k in range(1, 16)]
+                  + [(R(pb, 0, n), whole("NI16"), R(CF, i0, i1), False, True)])
             for j in range(0, 16, 4):
                 mm(bl[j:j + 4], "BX")
-            tt(R("M2", i0, i1), R("pB", 0, n), R("CR", i0, i1), OP.mult, 1.0, name="m2")
-            mm([(R("pB", 256, 256 + n), whole("ID16"), R("M2", i0, i1), True, False),
-                (R("pB", 256, 256 + n), whole("ID16"), R(CF, i0, i1), False, True)], "mend")
-            act(R("B", MEND + i0, MEND + i1), R("pB", 256, 256 + n), AF.Copy, name="mend")
+            tt(R("M2", i0, i1), R(pb, 0, n), R("CR", i0, i1), OP.mult, 1.0, name="m2")
+            mm([(R(pb, 256, 256 + n), whole("ID16"), R("M2", i0, i1), True, False),
+                (R(pb, 256, 256 + n), whole("ID16"), R(CF, i0, i1), False, True)], "mend")
+            act(R("B", MEND + i0, MEND + i1), R(pb, 256, 256 + n), AF.Copy, name="mend")
+        ck[0] = 9
 
         def wrap(bank, lh, src, name):
             mm([(R(bank, 0, 28), R(lh, 15 - b, 143 - b), R(src, b, L, 16), b == 0, b == 15) for b in range(16)], name)
-        wrap("pU0", "FW4", V, "h4")
-        tt(R("hbf", 0, 28), R("pU0", 0, 28), R("IB", 0, 28), OP.add, 1.0, name="hb")
-        sa, su, sl = c1("SA"), R("SUMS", 0, nc - 1), R("SUMS", nc - 1, nc)
+        wrap("pU0", "FW", V, "h")
+        cp(R("n1", 0, 28), R("pU0", 0, 28), name="h1")
+        ts(R("n2", 0, 28), R("n1", 0, 28), 2047, None, OP.bitwise_and, name="h2")
+        tt(R("hbf", 0, 28), R("n2", 0, 28), R("IB", 0, 28), OP.add, name="hb")
+        sa, su, sl = c1("SA"), R("SUMS", 0, nc), R("SUMS", nc, nc + 1)
         add("v", lambda g, T, X, sa=sa, su=su: g.vector.tensor_reduce(ap(T, sa), ap(T, su), AxisListType.X, OP.add), [su], [sa], vc(4), name="SA")
         mm([(R("pU2", 0, 1), whole("OB"), sa, True, False), (R("pU2", 0, 1), whole("OB"), sl, False, True)], "A", True)
         wrap("pU1", "F", "SG", "n")
         ts(R("rej", 0, 28), R("pU1", 0, 28), -5.0, 2048.0, OP.is_gt, OP.mult, name="rej")
-        ts(R("acc", 0, 28), R("pU1", 0, 28), -5.0, None, OP.is_lt, name="acc")
-        ts(R("t1", 0, 28), R("hbf", 0, 28), R("pU2", 0, 1), None, OP.add, name="t1")
+        act(R("acc", 0, 28), R("rej", 0, 28), AF.Identity, bias=c1("ONE"), scale=-1.0 / 2048, name="acc")
+        ts(R("t1", 0, 28), R("hbf", 0, 28), R("pU2", 0, 1), 512.0, OP.add, OP.mult, name="t1")
         ts(R("t2", 0, 28), R("t1", 0, 28), 2047, None, OP.bitwise_and, name="t2")
         tt(R("t3", 0, 28), R("t2", 0, 28), R("rej", 0, 28), OP.add, name="t3")
         cp(R(LS, 0, 28), R("t3", 0, 28), name="list")
         send("L", R(LS, 0, 14), R("rl%d" % t, 0, 14))
-        ts(c1("A1"), R("pU2", 0, 1), 1.0 / 512, 1536.0, OP.mult, OP.add, name="A1")
-        wrap("pE0", "FW", V, "h")
-        ts(R("n1", 0, 28), R("pE0", 0, 28), 37.0, c1("A1"), OP.mult, OP.add, name="n1")
-        ts(R("n2", 0, 28), R("n1", 0, 28), 2047, None, OP.bitwise_and, name="n2")
-        tt(R("n3", 0, 28), R("n2", 0, 28), R("acc", 0, 28), OP.mult, name="n3")
+        ts(R("n5", 0, 28), R("n2", 0, 28), 37.0, R("pU2", 0, 1), OP.mult, OP.add, name="n1")
+        ts(R("n6", 0, 28), R("n5", 0, 28), 2047, None, OP.bitwise_and, name="n2")
+        tt(R("n3", 0, 28), R("n6", 0, 28), R("acc", 0, 28), OP.mult, name="n3")
         tt(R("dl", 0, 28), R("rej", 0, 28), R("MC", 0, 28), OP.mult, name="dl")
         tt(R("n4", 0, 28), R("n3", 0, 28), R("dl", 0, 28), OP.add, name="n4")
         ts(R("NL", 0, 28), R("n4", 0, 28), 448.0, None, OP.add, name="NL")
@@ -361,7 +373,7 @@ def force(ops):
 
 def schedule(ops, deps):
     n = len(ops)
-    fc, adj, delta = force(ops), PLAN["adj"], PLAN["delta"]
+    fc, adj, dl, wf = force(ops), PLAN["adj"], PLAN["delta"], PLAN["wf"]
     succ = [[] for _ in range(n)]
     for i in range(n):
         for j in deps[i]:
@@ -369,7 +381,7 @@ def schedule(ops, deps):
     pri = [0.0] * n
     for i in range(n - 1, -1, -1):
         pri[i] = ops[i]["cost"] + max([pri[s] + LAT for s in succ[i]] or [0.0])
-    pri = [pri[i] + adj.get(ops[i]["name"], 0.0) for i in range(n)]
+    pa = [pri[i] + adj.get(ops[i]["name"], 0.0) + adj.get("%s@%d" % (ops[i]["name"], ops[i]["ck"]), 0.0) for i in range(n)]
     left = [len(d) for d in deps]
     ready = {i: 0.0 for i in range(n) if left[i] == 0}
     free = {"v": 0.0, "s": 0.0, "t": 0.0, "g": 0.0, "y": 0.0}
@@ -388,9 +400,13 @@ def schedule(ops, deps):
         if best is None:
             for q, c in heads.items():
                 t0 = min(c)[0]
-                st, i = max(c, key=lambda z: (z[0] <= t0 + delta, pri[z[1]], -z[1]))
-                if best is None or st < best[0]:
-                    best = (st, q, i)
+                if best is not None and t0 >= best[0]:
+                    continue
+                a = max((pa[i], -i) for st, i in c if st <= t0 + dl)
+                lim = t0 + max(dl, wf * ops[-a[1]]["cost"])
+                a = max((pa[i], -i, st) for st, i in c if st <= lim)
+                if best is None or a[2] < best[0]:
+                    best = (a[2], q, -a[1])
         st, q, i = best
         del ready[i]
         o = ops[i]
@@ -405,7 +421,7 @@ def schedule(ops, deps):
         for s in succ[i]:
             left[s] -= 1
             if left[s] == 0:
-                ready[s] = max(fin[j] + (LAT if deps[s][j] else 0.0) for j in deps[s])
+                ready[s] = max(fin[j] + (LAT if w else 0.0) for j, w in deps[s].items())
     return order, max(fin)
 
 

from concourse.mybir import AluOpType as OP, AxisListType, ActivationFunctionType as AF

N, NT = 4, 4
L, HB, W = 448, 224, 2048
CHUNKS = [(0, 96), (96, 128), (224, 128), (352, 96)]
PIECE = 64
MEND, BTAB = 0, 448
BW, XW = 448 + 4096, 4096
PLAN = {'x0': 'xsxxxxsx', 'x1': 'svvsxvss', 'r0': 'sssvssssxxssxs', 'r1': 'vxsssxsxssxxxs',
        'adj': {'BG': -31.6, 'v': -16.3, 'XG': -14.6, 'm2': 68.5, 'BX': -100.8, 'relu': 7.5, 'U': -34.2, 'E': 49.3, 'v0': 42.2,
                'abs': -28.5, 'copy': 7.2, 'A': 9.5, 'ZL': 17.7, 'relu@1': -14.9, 'd': 16.1, 'sign@1': -10.3, 'EL': -11.1,
                'v@1': 33.3, 'S16': 10.7, 'rej': -17.6, 'v@0': 10.2, 'abs@2': 35.9, 't2': -21.6, 'relu@2': 7.5, 'BX@2': -6.0,
                'BG@3': -27.0, 'BX@1': -6.5}, 'delta': 0.06, 'wf': 0.11}

F32, B16, I32, U16, H16 = "float32", "bfloat16", "int32", "uint16", "float16"
SCRATCH = {}
for _n, _w, _d in (
        ("X", XW, B16), ("B", BW, F32), ("pki", 1024, I32), ("tlo", 1024, I32), ("thi", 1024, I32), ("cbi", L, I32), ("wti", 8, I32),
        ("C0", L, U16), ("C1", L, U16), ("CF0", L, H16), ("CF1", L, H16), ("G", 16 * L, B16), ("GB", 16 * L, H16), ("R", 15 * L, B16),
        ("QI", L, I32), ("Y", L, B16), ("FT", 2 * L, B16), ("V0", L, B16), ("V1", L, B16), ("AB", L, B16), ("SG", L, B16),
        ("CR", L, B16), ("VT", 8 * 128, B16), ("M2", L, H16), ("YC", L, F32), ("SUMS", 8, F32), ("SA", 8, F32), ("hbf", 32, F32),
        ("rej", 32, F32), ("acc", 32, F32), ("t1", 32, I32), ("t2", 32, I32), ("t3", 32, F32), ("n1", 32, I32), ("n5", 32, I32),
        ("n6", 32, I32), ("n2", 32, I32), ("n3", 32, F32), ("n4", 32, F32), ("dl", 32, F32), ("LS0", 32, U16), ("LS1", 32, U16),
        ("NL", 32, U16), ("COL", 144, F32), ("KC", 128, F32), ("GC", 128, F32), ("M64", 128, F32), ("PI", 8, I32), ("PF", 8, F32),
        ("KI", 8, I32), ("GI", 8, I32), ("K8I", 8, I32), ("RGI", 8, I32), ("KF", 8, F32), ("GF", 8, F32), ("K8F", 8, F32),
        ("RGF", 8, F32), ("CFF", 8, F32), ("CBA", 8, F32), ("BIAS", 8, F32), ("P1", 8, F32), ("K2", 8, F32), ("NEG", 8, F32),
        ("ONE", 8, F32), ("HALF", 8, F32), ("KD", 8, F32), ("KLO", 8, F32), ("IB0", 32, F32), ("IB", 32, F32), ("MC0", 32, F32),
        ("MC", 32, F32), ("RM", 16, F32), ("RM8", 8, F32), ("ID", 128, B16), ("ID6", 128, B16), ("ID16", 128, H16),
        ("NI16", 128, H16), ("F", 144, B16), ("BA", 128, B16), ("DA", 128, B16), ("DB", 128, B16), ("EL", 15 * 128, B16),
        ("ZM", 128, B16), ("KV", 128, B16), ("ZB", 128, B16), ("ZL", 8 * 128, B16), ("S16", 16 * 128, H16), ("O8", 8, B16),
        ("O80", 8, B16), ("SH", 128, B16), ("KM", 128, B16), ("DF0", 128, B16), ("DF", 128, B16), ("OB", 128, F32), ("WF", 8, F32),
        ("FW", 144, B16)):
    SCRATCH[_n] = ("sbuf", [128, _w], _d)
for _t in range(NT):
    SCRATCH["rc%d" % _t] = ("sbuf", [128, HB], U16)
    SCRATCH["rv%d" % _t] = ("sbuf", [128, HB], B16)
    SCRATCH["rl%d" % _t] = ("sbuf", [128, 16], U16)
for _n in ("pE0", "pE1", "pU0", "pU1", "pU2", "pV", "pS", "pB"):
    SCRATCH[_n] = ("psum", [128, 512], F32)
SEMAPHORES = (["qv", "qs", "qt", "qg", "dcb", "dx", "dpk", "dwt", "oyx", "oyc"]
              + [a + b + str(t) for a in "rl" for b in "CVL" for t in range(NT)])

CY, TCY, GAM, SCA, LAT = 0.00083 * 1.15, 0.00042 * 1.15, 1.4, 3, 0.1


def R(buf, c0, c1, step=1, p0=0, p1=128):
    return (buf, c0, c1, step, p0, p1)


def ap(T, a):
    buf, c0, c1, step, p0, p1 = a
    if step == 1:
        return T[buf][p0:p1, c0:c1]
    return T[buf][p0:p1, c0:c1:step]


def val(T, s):
    return ap(T, s) if isinstance(s, tuple) else s


def build_ops(nsig):
    ops, ck = [], [9]

    def add(eng, fn, reads, writes, cost, tok=None, name="", after=()):
        ops.append(dict(eng=eng, fn=fn, reads=list(reads), writes=list(writes), cost=cost, tok=tok, name=name, after=list(after), ck=ck[0]))
        return len(ops) - 1

    def ne(a):
        return -((a[1] - a[2]) // a[3])

    def vc(n):
        return 0.06 + max(64, n) * CY

    def cp(out, in_, cyc=1.0, name="copy"):
        add("v", lambda g, T, X: g.vector.tensor_copy(ap(T, out), ap(T, in_)), [in_], [out], vc(ne(out) * cyc), name=name)

    def ts(out, in0, s1, s2, op0, op1=None, cyc=1.0, name="ts"):
        def fn(g, T, X):
            if op1 is None:
                return g.vector.tensor_scalar(ap(T, out), ap(T, in0), val(T, s1), None, op0)
            return g.vector.tensor_scalar(ap(T, out), ap(T, in0), val(T, s1), val(T, s2), op0, op1)
        add("v", fn, [in0] + [s for s in (s1, s2) if isinstance(s, tuple)], [out], vc(ne(out) * cyc), name=name)

    def tt(out, a, b, op, cyc=2.0, name="tt"):
        add("v", lambda g, T, X: g.vector.tensor_tensor(ap(T, out), ap(T, a), ap(T, b), op), [a, b], [out], vc(ne(out) * cyc), name=name)

    def ms(out, x):
        add("v", lambda g, T, X: g.vector.memset(ap(T, out), x), [], [out], vc(ne(out)), name="memset")

    def act(out, in_, func, bias=0.0, scale=1.0, accum=None, name="act"):
        def fn(g, T, X):
            if accum is None:
                return g.scalar.activation(ap(T, out), ap(T, in_), func, bias=val(T, bias), scale=val(T, scale))
            return g.scalar.activation(ap(T, out), ap(T, in_), func, bias=val(T, bias), scale=val(T, scale), accum_out=ap(T, accum))
        add("s", fn, [in_] + [s for s in (bias, scale) if isinstance(s, tuple)], [out] + ([accum] if accum else []), 0.08 + ne(out) * CY, name=name)

    def gat(eng, out, win, off, name):
        def fv(g, T, X):
            return g.vector.tensor_copy(ap(T, out), ap(T, win).indirect(ap(T, off)))

        def fs(g, T, X):
            return g.scalar.activation(ap(T, out), ap(T, win).indirect(ap(T, off)), AF.Copy)
        add(eng, {"v": fv, "s": fs}, [win, off], [out], 0.06 + ne(out) * GAM * CY, name=name)

    def sca(win, off, in_, name):
        add("v", lambda g, T, X: g.vector.tensor_copy(ap(T, win).indirect(ap(T, off)), ap(T, in_)), [in_, off], [win],
            0.06 + ne(in_) * SCA * CY, name=name)

    def mm(lst, name, f32=False):
        def fn(g, T, X):
            i = None
            for o, l, r, a, b in lst:
                i = g.tensor.matmul(ap(T, o), ap(T, l), ap(T, r), a, b)
            return i
        cost = sum(max(64, ne(r)) for _o, _l, r, _a, _b in lst) * TCY * (4 if f32 else 1)
        add("t", fn, [x for m in lst for x in (m[1], m[2])], [m[0] for m in lst], 0.05 + cost, name=name)

    def iota(out, pat, base, cm, f32=True):
        def fn(g, T, X):
            if f32:
                return g.iota(ap(T, out), pat, base, cm, allow_small_or_imprecise_dtypes=True)
            return g.iota(ap(T, out), pat, base, cm)
        add("g", fn, [], [out], 0.15 + 2 * ne(out) * CY, name="iota")

    def c1(b):
        return R(b, 0, 1)

    def whole(b):
        return R(b, 0, SCRATCH[b][1][1])

    def scaled(o, base, col, name):
        def fv(g, T, X):
            return g.vector.tensor_scalar(ap(T, o), ap(T, base), ap(T, col), None, OP.mult)

        def fs(g, T, X):
            return g.scalar.activation(ap(T, o), ap(T, base), AF.Copy, scale=ap(T, col))
        add("vs", {"v": fv, "s": fs}, [base, col], [o], 0.12, name=name)

    add("y", lambda g, T, X: g.sync.dma_start(T.cbi[:, :], T.cb[:, :]), [], [R("cbi", 0, L)], 2.5, ("dcb", 16), "ld cb")
    add("sd", lambda g, T, X: g.scalar.dma_start(T.X[:, 0:W], T.x[:, :]), [], [R("X", 0, W)], 4.5, ("dx", 16), "ld x")
    add("y", lambda g, T, X: g.sync.dma_start(T.wti[:, 0:1], T.wt[:, :]), [], [c1("wti")], 2.0, ("dwt", 16), "ld wt")
    add("y", lambda g, T, X: g.sync.dma_start(T.pki[:, :], T.pk[:, :]), [], [R("pki", 0, 1024)], 4.5, ("dpk", 16), "ld pk")
    iota(c1("PI"), [[1, 1]], 0, 1, False)
    iota(c1("PF"), [[1, 1]], 0, 1)
    iota(R("M64", 0, 128), [[0, 2], [1, 64]], 0, 0)
    iota(R("COL", 0, 144), [[1, 144]], 0, 0)
    iota(R("GC", 0, 128), [[1, 8], [0, 16]], 0, 0)
    iota(R("KC", 0, 128), [[0, 8], [1, 16]], 0, 0)
    iota(R("IB0", 0, 14), [[32, 14]], 1, 0)
    iota(R("IB0", 14, 28), [[32, 14]], 0, 0)
    iota(R("MC0", 0, 28), [[16, 28]], -448, 0)
    ts(c1("KI"), c1("PI"), 15, None, OP.bitwise_and)
    ts(c1("GI"), c1("PI"), 4, None, OP.logical_shift_right)
    ts(c1("K8I"), c1("PI"), 7, None, OP.bitwise_and)
    ts(c1("RGI"), c1("PI"), 63, 3, OP.bitwise_and, OP.logical_shift_right)
    cp(c1("KF"), c1("KI"))
    cp(c1("GF"), c1("GI"))
    cp(c1("K8F"), c1("K8I"))
    cp(c1("RGF"), c1("RGI"))
    cp(R("C0", 0, HB), R("cbi", 1, L, 2), name="c16")
    cp(R("C0", HB, L), R("cbi", 0, L, 2), name="c16")
    ts(c1("CBA"), c1("GF"), 8.0, c1("K8F"), OP.mult, OP.add)
    ts(whole("ID6"), R("COL", 0, 128), c1("PF"), 0.0625, OP.is_equal, OP.mult)
    ts(whole("BA"), whole("M64"), c1("CBA"), None, OP.is_equal)
    ts(R("RM", 0, 16), R("COL", 0, 16), c1("KF"), None, OP.is_equal)
    for k in range(15):
        scaled(R("EL", 128 * k, 128 * k + 128), whole("ID6"), R("RM", k, k + 1), "EL")
    ts(whole("ID"), R("COL", 0, 128), c1("PF"), None, OP.is_equal)
    ts(c1("KLO"), c1("KF"), 7.5, None, OP.is_lt)
    ts(c1("KD"), c1("KF"), 7.5, None, OP.is_gt)
    scaled(whole("DA"), whole("BA"), c1("KLO"), "DA")
    scaled(whole("DB"), whole("BA"), c1("KD"), "DA")
    ms(R("HALF", 0, 1, 1, 0, 64), 0.0)
    ms(R("HALF", 0, 1, 1, 64, 128), -0.5)
    ts(R("RM8", 0, 8), R("COL", 0, 8), c1("K8F"), None, OP.is_equal)
    ts(whole("ZM"), whole("GC"), c1("RGF"), None, OP.is_equal)
    ts(R("KV", 0, 128, 1, 0, 64), R("KC", 0, 128, 1, 0, 64), 8192.0, -65536.0, OP.mult, OP.add)
    ts(R("KV", 0, 128, 1, 64, 128), R("KC", 0, 128, 1, 64, 128), -8192.0, None, OP.mult)
    tt(whole("ZB"), whole("ZM"), whole("KV"), OP.mult)
    for s in range(8):
        scaled(R("ZL", 128 * s, 128 * s + 128), whole("ZB"), R("RM8", s, s + 1), "ZL")
    ts(c1("K2"), c1("KF"), -256.0, 2048.0, OP.mult, OP.add)
    tt(c1("BIAS"), c1("KF"), c1("K2"), OP.mult)
    ts(c1("CFF"), c1("GF"), 16.0, 15.0, OP.mult, OP.add)
    ts(whole("F"), whole("COL"), c1("CFF"), None, OP.is_equal)
    ts(R("O8", 0, 8), R("COL", 0, 8), c1("GF"), None, OP.is_equal)
    ts(R("O80", 0, 8), R("O8", 0, 8), R("RM", 0, 1), None, OP.mult)
    ts(c1("P1"), c1("PF"), 1.0, None, OP.add)
    ts(whole("SH"), R("COL", 0, 128), c1("P1"), None, OP.is_equal)
    tt(whole("DF0"), whole("ID"), whole("SH"), OP.subtract)
    ts(whole("KM"), whole("KC"), 0.0, None, OP.is_gt)
    tt(whole("DF"), whole("DF0"), whole("KM"), OP.mult)
    ms(c1("NEG"), -80.5)
    ms(c1("ONE"), 1.0)
    ms(c1("SUMS"), 448.0)
    cp(c1("WF"), c1("wti"))
    scaled(whole("FW"), whole("F"), c1("WF"), "FW")
    ts(whole("OB"), whole("GC"), c1("GF"), 0.5, OP.is_equal, OP.mult)
    ts(c1("K2"), c1("KF"), 2.0, None, OP.mult)
    ts(R("IB", 0, 28), R("IB0", 0, 28), c1("K2"), 1.0 / 512, OP.add, OP.mult)
    ts(R("MC", 0, 28), R("MC0", 0, 28), c1("KF"), 1.0 / 2048, OP.add, OP.mult)
    ts(whole("ID16"), R("COL", 0, 128), c1("PF"), None, OP.is_equal)
    ts(whole("NI16"), whole("ID16"), -1.0, None, OP.mult)
    for k in range(1, 16):
        ts(R("S16", 128 * k, 128 * k + 128), whole("ID16"), R("RM", k, k + 1), None, OP.mult, cyc=0.5, name="S16")
    ts(whole("tlo"), whole("pki"), W - 1, None, OP.bitwise_and)
    cp(R("B", BTAB, BTAB + 1024), whole("tlo"))
    ts(whole("thi"), whole("pki"), 11, None, OP.logical_shift_right)
    cp(R("B", BTAB + 1024, BTAB + 2048), whole("thi"))
    cp(whole("CF0"), whole("C0"), 0.5)

    xw, bw = R("X", 0, W), R("B", BTAB, BTAB + W)
    ub, un = ["pU0", "pU1", "pU2"], 0
    nc = len(CHUNKS)

    for t in range(NT):
        C, CF, V, LS = "C%d" % (t % 2), "CF%d" % (t % 2), "V%d" % (t % 2), "LS%d" % (t % 2)

        def send(what, src, dst, t=t):
            def fn(g, T, X):
                rid, pid, m = X[t]
                return g.remote_dma(ap(T, dst), ap(T, src), T.sem["r%s%d" % (what, t)], T.sem["l%s%d" % (what, t)], pid, rid, m)
            i = add("g", fn, [src], [], 0.6, ("l%s%d" % (what, t), nsig), "send " + what)
            add("x", None, [], [dst], 2.2, ("r%s%d" % (what, t), nsig), "recv " + what, [i])

        send("C", R(C, 0, HB), R("rc%d" % t, 0, HB))
        for c, (i0, n) in enumerate(CHUNKS):
            i1, g0, ck[0] = i0 + n, 16 * i0, c
            for j in range(i0, i1, PIECE):
                e = min(j + PIECE, i1)
                gat("vs", R("G", 16 * j, 16 * e), xw, R(C, j, e), "XG")
            pe = "pE%d" % (c % 2)
            mm([(R(pe, 0, n), R("EL", 128 * k, 128 * k + 128), R("G", g0 + k, 16 * i1, 16), k == 0, k == 14) for k in range(15)], "E")
            q, y = R("QI", i0, i1), R("Y", i0, i1)
            ts(q, R(pe, 0, n), 0.46875, None, OP.subtract, name="q")
            tt(y, R(pe, 0, n), q, OP.subtract, 1.0, name="y")
            mm([(R(pe, 256, 256 + n), whole("DA"), y, True, True), (R(pe, 256 + n, 256 + 2 * n), whole("DB"), y, True, True)], "yy")
            act(R("FT", 2 * i0, 2 * i1), R(pe, 256, 256 + 2 * n), AF.Square, bias=c1("HALF"), name="sq")
            mm([(R("pV", 0, 128, 16, 0, n), R("G", g0, 16 * i1, 16), R("O80", 0, 8), True, True)], "v0")
            per = 512 // n
            for b in range(0, 15, per):
                kk = list(range(1, 16))[b:b + per]
                u = ub[un % 3]
                un += 1
                lst = []
                for x, k in enumerate(kk):
                    o, s, h = R(u, x * n, x * n + n), (k - 1) % 8, (k - 1) // 8
                    lst.append((o, whole("ID"), R("G", g0 + k, 16 * i1, 16), True, False))
                    lst.append((o, R("ZL", 128 * s, 128 * s + 128), R("FT", 2 * i0 + h * n, 2 * i0 + h * n + n), False, True))
                mm(lst, "U")
                r0 = 15 * i0 + b * n
                ro, ui = R("R", r0, r0 + len(kk) * n), R(u, 0, len(kk) * n)

                def fv(g, T, X, ro=ro, ui=ui):
                    return g.vector.tensor_scalar(ap(T, ro), ap(T, ui), T.BIAS[:, 0:1], 0.0, OP.add, OP.max)

                def fs(g, T, X, ro=ro, ui=ui):
                    return g.scalar.activation(ap(T, ro), ap(T, ui), AF.Relu, bias=T.BIAS[:, 0:1])
                add("vs", {"v": fv, "s": fs}, [ui, c1("BIAS")], [ro], 0.08 + len(kk) * n * CY, name="relu")
                mm([(R("pV", k, 128, 16, 0, n), R("R", 15 * i0 + (k - 1) * n, 15 * i0 + k * n), R("O8", 0, 8), True, True) for k in kk], "v")
            vv, vt = R(V, i0, i1), R("VT", 128 * c, 128 * c + 128, 1, 0, n)
            act(vt, R("pV", 0, 128, 1, 0, n), AF.Copy, name="vt")
            mm([(R("pS", 128, 128 + n), vt, R("ID", 0, n, 1, 0, n), True, True)], "vn")
            act(vv, R("pS", 128, 128 + n), AF.Copy, name="vcopy")
            mm([(R("pS", 0, n), whole("DF"), vv, True, True)], "d")
            act(R("AB", i0, i1), R("pS", 0, n), AF.Abs, name="abs")
            act(R("SG", i0, i1), R("AB", i0, i1), AF.Sign, bias=c1("NEG"), accum=R("SUMS", c + 1, c + 2), name="sign")
            act(R("CR", i0, i1), R("SG", i0, i1), AF.Relu, name="cr")
            if i1 == HB:
                send("V", R(V, 0, HB), R("rv%d" % t, 0, HB))
        for c, (i0, n) in enumerate(CHUNKS):
            i1, g0, ck[0], pb = i0 + n, 16 * i0, c, ("pB", "pV", "pE1", "pS")[c]
            for j in range(i0, i1, PIECE):
                e = min(j + PIECE, i1)
                gat("v", R("GB", 16 * j, 16 * e), bw, R(C, j, e), "BG")
            bl = ([(R(pb, 0, n), R("S16", 128 * k, 128 * k + 128), R("GB", g0 + k, 16 * i1, 16), k == 1, False) for k in range(1, 16)]
                  + [(R(pb, 0, n), whole("NI16"), R(CF, i0, i1), False, True)])
            for j in range(0, 16, 4):
                mm(bl[j:j + 4], "BX")
            tt(R("M2", i0, i1), R(pb, 0, n), R("CR", i0, i1), OP.mult, 1.0, name="m2")
            mm([(R(pb, 256, 256 + n), whole("ID16"), R("M2", i0, i1), True, False),
                (R(pb, 256, 256 + n), whole("ID16"), R(CF, i0, i1), False, True)], "mend")
            act(R("B", MEND + i0, MEND + i1), R(pb, 256, 256 + n), AF.Copy, name="mend")
        ck[0] = 9

        def wrap(bank, lh, src, name):
            mm([(R(bank, 0, 28), R(lh, 15 - b, 143 - b), R(src, b, L, 16), b == 0, b == 15) for b in range(16)], name)
        wrap("pU0", "FW", V, "h")
        cp(R("n1", 0, 28), R("pU0", 0, 28), name="h1")
        ts(R("n2", 0, 28), R("n1", 0, 28), 2047, None, OP.bitwise_and, name="h2")
        tt(R("hbf", 0, 28), R("n2", 0, 28), R("IB", 0, 28), OP.add, name="hb")
        sa, su, sl = c1("SA"), R("SUMS", 0, nc), R("SUMS", nc, nc + 1)
        add("v", lambda g, T, X, sa=sa, su=su: g.vector.tensor_reduce(ap(T, sa), ap(T, su), AxisListType.X, OP.add), [su], [sa], vc(4), name="SA")
        mm([(R("pU2", 0, 1), whole("OB"), sa, True, False), (R("pU2", 0, 1), whole("OB"), sl, False, True)], "A", True)
        wrap("pU1", "F", "SG", "n")
        ts(R("rej", 0, 28), R("pU1", 0, 28), -5.0, 2048.0, OP.is_gt, OP.mult, name="rej")
        act(R("acc", 0, 28), R("rej", 0, 28), AF.Identity, bias=c1("ONE"), scale=-1.0 / 2048, name="acc")
        ts(R("t1", 0, 28), R("hbf", 0, 28), R("pU2", 0, 1), 512.0, OP.add, OP.mult, name="t1")
        ts(R("t2", 0, 28), R("t1", 0, 28), 2047, None, OP.bitwise_and, name="t2")
        tt(R("t3", 0, 28), R("t2", 0, 28), R("rej", 0, 28), OP.add, name="t3")
        cp(R(LS, 0, 28), R("t3", 0, 28), name="list")
        send("L", R(LS, 0, 14), R("rl%d" % t, 0, 14))
        ts(R("n5", 0, 28), R("n2", 0, 28), 37.0, R("pU2", 0, 1), OP.mult, OP.add, name="n1")
        ts(R("n6", 0, 28), R("n5", 0, 28), 2047, None, OP.bitwise_and, name="n2")
        tt(R("n3", 0, 28), R("n6", 0, 28), R("acc", 0, 28), OP.mult, name="n3")
        tt(R("dl", 0, 28), R("rej", 0, 28), R("MC", 0, 28), OP.mult, name="dl")
        tt(R("n4", 0, 28), R("n3", 0, 28), R("dl", 0, 28), OP.add, name="n4")
        ts(R("NL", 0, 28), R("n4", 0, 28), 448.0, None, OP.add, name="NL")
        xs, bs = R("X", 0, XW), R("B", BTAB, BW)
        ls, rl = R(LS, 14, 28), R("rl%d" % t, 0, 14)
        sca(xs, ls, R(V, HB, L), "XS even")
        sca(bs, ls, R(C, HB, L), "BS even")
        last = t == NT - 1
        rest = [(xs, R("rv%d" % t, 0, HB), "XS odd"), (bs, R("rc%d" % t, 0, HB), "BS odd")]
        for w, s, nm in (rest if last else rest[::-1]):
            sca(w, rl, s, nm)
        bn = R("B", 0, BTAB + W)
        if last:
            add("y", lambda g, T, X: g.sync.dma_start(T.yx[:, :], T.X[:, 0:W]), [R("X", 0, W)], [], 4.0, ("oyx", 16), "st x")
            gat("v", R("YC", 1, L, 2), bn, R("NL", 0, 14), "nxt")
            gat("s", R("YC", 0, L, 2), bn, R("NL", 14, 28), "nxt")
            add("y", lambda g, T, X: g.sync.dma_start(T.yc[:, :], T.YC[:, :]), [R("YC", 0, L)], [], 2.5, ("oyc", 16), "st c")
        else:
            D, DF_ = "C%d" % ((t + 1) % 2), "CF%d" % ((t + 1) % 2)
            gat("v", R(D, 0, HB), bn, R("NL", 0, 14), "nxt")
            gat("v", R(D, HB, L), bn, R("NL", 14, 28), "nxt")
            cp(whole(DF_), whole(D), 0.5, name="cf")
    return ops


def hit(a, b):
    return a[0] == b[0] and a[1] < b[2] and b[1] < a[2] and a[4] < b[5] and b[4] < a[5]


def depend(ops):
    hist, deps = {}, []
    for i, o in enumerate(ops):
        d = {a: True for a in o["after"]}
        acc = [(r, False) for r in o["reads"]] + [(w, True) for w in o["writes"]]
        for r, wr in acc:
            ps = SCRATCH[r[0]][0] == "psum"
            for j, q, qw in hist.get(r[0], []):
                if j == i:
                    continue
                same = ops[j]["eng"] == o["eng"] and o["eng"] in ("t", "v", "s", "g")
                over = hit(r, q) and (wr or qw)
                if same and o["eng"] == "t":
                    if over:
                        d[j] = d.get(j, False)
                elif over or (ps and not same):
                    d[j] = True
        deps.append(d)
        for r, wr in acc:
            h = hist.setdefault(r[0], [])
            if wr and SCRATCH[r[0]][0] != "psum" and r[3] == 1:
                h[:] = [e for e in h if e[0] == i or not (e[1][1] >= r[1] and e[1][2] <= r[2] and e[1][4] >= r[4] and e[1][5] <= r[5])]
            h.append((i, r, wr))
            if SCRATCH[r[0]][0] == "psum":
                del h[:-80]
    return deps


def force(ops):
    f, k = {}, {"XG": 0, "relu": 0}
    tot = {z: sum(o["name"] == z for o in ops) // NT for z in k}
    for i, o in enumerate(ops):
        z = o["name"]
        if z in k:
            f[i] = PLAN[("x" if z == "XG" else "r") + ("0" if k[z] < tot[z] else "1")][k[z] % tot[z]]
            k[z] += 1
    return {i: ("vs" if v == "x" else v) for i, v in f.items()}


def schedule(ops, deps):
    n = len(ops)
    fc, adj, dl, wf = force(ops), PLAN["adj"], PLAN["delta"], PLAN["wf"]
    succ = [[] for _ in range(n)]
    for i in range(n):
        for j in deps[i]:
            succ[j].append(i)
    pri = [0.0] * n
    for i in range(n - 1, -1, -1):
        pri[i] = ops[i]["cost"] + max([pri[s] + LAT for s in succ[i]] or [0.0])
    pa = [pri[i] + adj.get(ops[i]["name"], 0.0) + adj.get("%s@%d" % (ops[i]["name"], ops[i]["ck"]), 0.0) for i in range(n)]
    left = [len(d) for d in deps]
    ready = {i: 0.0 for i in range(n) if left[i] == 0}
    free = {"v": 0.0, "s": 0.0, "t": 0.0, "g": 0.0, "y": 0.0}
    fin, order = [0.0] * n, []
    while ready:
        best, heads = None, {}
        for i, r in ready.items():
            e = ops[i]["eng"]
            if e == "x":
                best = (r, "x", i)
                break
            if e == "vs":
                e = fc.get(i, "vs")
            for q in ("v", "s") if e == "vs" else (("s",) if e == "sd" else (e,)):
                heads.setdefault(q, []).append((max(free[q], r), i))
        if best is None:
            for q, c in heads.items():
                t0 = min(c)[0]
                if best is not None and t0 >= best[0]:
                    continue
                a = max((pa[i], -i) for st, i in c if st <= t0 + dl)
                lim = t0 + max(dl, wf * ops[-a[1]]["cost"])
                a = max((pa[i], -i, st) for st, i in c if st <= lim)
                if best is None or a[2] < best[0]:
                    best = (a[2], q, -a[1])
        st, q, i = best
        del ready[i]
        o = ops[i]
        if q == "x":
            fin[i] = st + o["cost"]
        elif o["eng"] in ("y", "sd"):
            free[q] = st + 0.1
            fin[i] = st + o["cost"]
        else:
            free[q] = fin[i] = st + o["cost"]
        order.append((i, q))
        for s in succ[i]:
            left[s] -= 1
            if left[s] == 0:
                ready[s] = max(fin[j] + (LAT if w else 0.0) for j, w in deps[s].items())
    return order, max(fin)


_plan = {}


def plan(nsig):
    if nsig in _plan:
        return _plan[nsig]
    ops = build_ops(nsig)
    deps = depend(ops)
    order, span = schedule(ops, deps)
    sem = {"v": "qv", "s": "qs", "t": "qt", "g": "qg"}
    cnt, known, tok, snap, out = {}, {q: {} for q in "vstgy"}, {}, {}, []
    for i, q in order:
        o = ops[i]
        if q == "x":
            tok[i] = o["tok"]
            cnt[o["tok"][0]] = o["tok"][1]
            snap[i] = {o["tok"][0]: o["tok"][1]}
            continue
        kn, top = known[q], {}
        for j in sorted((j for j, w in deps[i].items() if w), reverse=True):
            s, v = tok[j]
            if kn.get(s, 0) < v:
                top[s] = max(top.get(s, 0), v)
                for a, b in snap[j].items():
                    if kn.get(a, 0) < b:
                        kn[a] = b
        if o["tok"]:
            tok[i] = o["tok"]
            cnt[o["tok"][0]] = o["tok"][1]
        else:
            s = sem[q]
            cnt[s] = cnt.get(s, 0) + 1
            tok[i] = (s, cnt[s])
        snap[i] = dict(kn)
        snap[i][tok[i][0]] = tok[i][1]
        out.append((q, o, sorted(top.items()), tok[i]))
    _plan[nsig] = (out, cnt, span)
    return _plan[nsig]


def rank_program(g, core, T, topo):
    rank = T.rank_of(core)
    if rank is None:
        return
    X = []
    for t in range(NT):
        d = T.cores[(rank + 1 + t % (N - 1)) % N]
        rid, pid = topo.addr(d, core)
        X.append((rid, pid, topo.mask(core, d)))
    out, cnt, _span = plan(len(topo.engines(core, T.cores[(rank + 1) % N])))
    queue = {"v": g.vector, "s": g.scalar, "t": g.tensor, "g": g, "y": g.sync}
    for q, o, waits, tk in out:
        for s, v in waits:
            queue[q].wait_ge(T.sem[s], v)
        fn = o["fn"][q] if isinstance(o["fn"], dict) else o["fn"]
        ins = fn(g, T, X)
        if o["tok"] is None:
            ins.then_inc(T.sem[tk[0]], 1)
        elif o["name"][:4] != "send":
            ins.then_inc(T.sem[tk[0]], tk[1])
    for s, v in sorted(cnt.items()):
        g.wait_ge(T.sem[s], v)
